import numpy as np
import ml_dtypes


def mxq(x, axis, fmt="e4m3"):
    dtype, down = {"e4m3": (ml_dtypes.float8_e4m3fn, 7), "e5m2": (ml_dtypes.float8_e5m2, 14)}[fmt]
    v = np.moveaxis(np.asarray(x, np.float32).astype(ml_dtypes.bfloat16).astype(np.float64), axis, -1)
    blocks = v.reshape(v.shape[:-1] + (-1, 32))
    amax = np.abs(blocks).max(-1, keepdims=True)
    byte = np.maximum(np.where(amax > 0, np.frexp(amax)[1] - 1 + 127, 0) - down, 1)
    scale = np.exp2(byte - 127.0)
    codes = (blocks / scale).astype(np.float32).astype(dtype).astype(np.float64)
    return np.moveaxis((codes * scale).reshape(v.shape), -1, axis)


WIDE = False


def mx_kscale(k):
    if not WIDE:
        return np.ones(k)
    levels = np.array([10, -10, 5, -5, 0])
    if k % 512:
        return np.exp2(np.random.permutation(np.resize(levels, k // 32))).repeat(32)
    a = np.empty((k // 512, 16))
    for p in range(k // 512):
        a[p, :8] = np.random.permutation(np.resize(levels, 8))
        for g in range(8):
            far = levels[np.abs(levels - a[p, g]) >= 10]
            a[p, g + 8] = far[np.random.randint(len(far))]
    return np.exp2(a.ravel()).repeat(32)


def f64(x):
    return np.asarray(x).astype(np.float64)


def striped(idx):
    return np.tile(np.asarray(idx).reshape(-1, 16).T, (8, 1)).astype(np.uint16)


def unstriped(offs):
    return offs[:16].T.reshape(-1).astype(np.int64)


E2M1 = np.array([0.0, 0.5, 1.0, 1.5, 2.0, 3.0, 4.0, 6.0, -0.0, -0.5, -1.0, -1.5, -2.0, -3.0, -4.0, -6.0])


def pack_weight(w, fmt):
    k, n = w.shape
    w = f64(np.asarray(w, np.float32).astype(ml_dtypes.bfloat16)).reshape(k // 32, 32, n)
    amax = np.abs(w).max(1)
    if fmt == "e4m3":
        byte = np.frexp(amax)[1] - 1 + 127 - 7
    else:
        mant, ex = np.frexp(amax / 6.0)
        byte = np.where(mant > 0.5, ex, ex - 1) + 127
    byte = np.clip(np.where(amax > 0, byte, 1), 1, 254)
    scaled = (w * np.exp2(127.0 - byte)[:, None, :]).reshape(k, n).astype(np.float32)
    by_word = np.ascontiguousarray(scaled.reshape(k // 512, 128, 4, n).transpose(0, 1, 3, 2))
    if fmt == "e4m3":
        words = by_word.astype(ml_dtypes.float8_e4m3fn).view(np.uint8)
    else:
        c = by_word.astype(ml_dtypes.float4_e2m1fn).view(np.uint8) & 0xF
        words = (c[..., 0::2] | (c[..., 1::2] << 4)).reshape(k // 512, 128, 2 * n)
    return np.ascontiguousarray(words), np.ascontiguousarray(byte.astype(np.uint8).reshape(k // 512, 16, n))


def unpack_weight(words, scales, fmt):
    g, _, n = scales.shape
    words = np.ascontiguousarray(words).reshape(g, 128, n, -1)
    if fmt == "e4m3":
        vals = words.view(ml_dtypes.float8_e4m3fn).astype(np.float64)
    else:
        nib = np.empty((g, 128, n, 4), np.uint8)
        nib[..., 0::2] = words & 0xF
        nib[..., 1::2] = words >> 4
        vals = E2M1[nib]
    vals = vals * np.repeat(np.exp2(scales.astype(np.float64) - 127.0), 8, axis=1)[..., None]
    return vals.transpose(0, 1, 3, 2).reshape(g * 512, n)


D, T, I, J, U, E, Y = 512, 2048, 512, 512, 1024, 512, 1024


def setup_inputs():
    n = np.random.standard_normal
    idx = np.random.permutation(T)[:I]
    idx2 = np.random.permutation(U)[:J]
    idx3 = np.random.permutation(Y)[:I]
    fd = mx_kscale(D)
    fi = mx_kscale(I)
    ti = np.ones(T)
    ti[idx] = fi
    ti3 = np.ones(Y)
    ti3[idx3] = fi
    keysp = pack_weight(n((D, T)) / fd[:, None], "e4m3")
    return {
        "keys_words": keysp[0],
        "keys_scales": keysp[1],
        "notes": (n((D, U)) * 1.0 / np.sqrt(D) * fd[:, None]).astype(np.float32),
        "rowf": (np.random.uniform(0.02, 0.08, (I, 1)) * fi[:, None]).astype(np.float32),
        "rowf2": (np.random.uniform(0.02, 0.08, (I, 1)) * fi[:, None]).astype(np.float32),
        "vals": (n((E, T)) / ti).astype(np.float32),
        "vals2": (n((E, Y)) / ti3).astype(np.float32),
        "offs": striped(idx),
        "offs2": striped(idx2),
        "offs3": striped(idx3),
    }


def reference(keys_words, keys_scales, notes, rowf, rowf2, vals, vals2, offs, offs2, offs3):
    idx = unstriped(offs)
    idx2 = unstriped(offs2)
    idx3 = unstriped(offs3)
    keysu = unpack_weight(keys_words, keys_scales, "e4m3")
    keysidxg = keysu[:, idx]
    notesidx2q = mxq(f64(notes)[:, idx2], 0, "e4m3")
    g9 = keysidxg.T @ notesidx2q
    g0 = np.maximum(g9, 0.0)
    gr1 = g0 * f64(rowf)
    gr2 = g0 * f64(rowf2)
    vt1 = f64(vals)[:, idx].T
    vt2 = f64(vals2)[:, idx3].T
    vt1q = mxq(vt1, 0, "e4m3")
    gr1q = mxq(gr1, 0, "e4m3")
    vt2q = mxq(vt2, 0, "e4m3")
    gr2q = mxq(gr2, 0, "e4m3")
    o = vt1q.T @ gr1q + vt2q.T @ gr2q
    return o

@@ -1,0 +1,242 @@
+from contextlib import ExitStack
+
+import concourse.mybir as mybir
+from concourse.masks import make_identity
+
+F32 = mybir.dt.float32
+BF16 = mybir.dt.bfloat16
+I32 = mybir.dt.int32
+U32 = mybir.dt.uint32
+U16 = mybir.dt.uint16
+U8 = mybir.dt.uint8
+FP8X4 = mybir.dt.float8_e4m3fn_x4
+COPY = mybir.ActivationFunctionType.Copy
+ALU = mybir.AluOpType
+
+P = 128
+PACK = 4
+N = 512
+T, U, Y = 2048, 1024, 1024
+BLOCKS = N // P
+
+FLOPS = 3 * 2 * N * N * N
+
+
+def gather(nc, on_vector, out, window, offsets):
+    if on_vector:
+        nc.vector.tensor_copy(out, window.indirect(offsets))
+    else:
+        nc.scalar.activation(out, window.indirect(offsets), COPY)
+
+
+def quantise(nc, words, scales, woven):
+    nc.vector.quantize_mx(out=words.bitcast(FP8X4), scales=scales, in_=woven)
+
+
+def tile_attend_tab_plain_twostores_kernel(
+    tc, keys_words, keys_scales, notes, rowf, rowf2, vals, vals2, offs, offs2, offs3, out
+):
+    nc = tc.nc
+    with ExitStack() as ctx:
+        keep = ctx.enter_context(tc.tile_pool(name="keep", bufs=1))
+        psum = ctx.enter_context(tc.psum_pool(name="psum", bufs=1))
+
+        def bank(number, shape, name):
+            return psum.tile(shape, F32, name=name, tag="bank%d" % number)
+
+        def staged(tag, shape, dtype, name):
+            return keep.tile(shape, dtype, name=name, tag=tag, align_bytes=64)
+
+        list1 = keep.tile([P, N // 16], U16, name="list1")
+        list2 = keep.tile([P, N // 16], U16, name="list2")
+        list3 = keep.tile([P, N // 16], U16, name="list3")
+        note_pool = [keep.tile([P, U], F32, name="note_pool%d" % t) for t in range(PACK)]
+        key_pool = staged("key_pool", [P, T], U32, "key_pool")
+        key_scale_pool = keep.tile([P, T], U8, name="key_scale_pool")
+        val_pool = [staged("val_pool%d" % b, [P, T], F32, "val_pool%d" % b) for b in range(BLOCKS)]
+        val2_pool = [keep.tile([P, Y], F32, name="val2_pool%d" % b) for b in range(BLOCKS)]
+        factor1 = keep.tile([P, PACK], F32, name="factor1")
+        factor2 = keep.tile([P, PACK], F32, name="factor2")
+        ident = keep.tile([P, P], F32, name="ident")
+
+        nc.gpsimd.memset(key_scale_pool[:].bitcast(I32), 0)
+        note_planes = notes.rearrange("(p t) u -> t p u", t=PACK)
+        nc.sync.dma_start(list2[:], offs2)
+        nc.sync.dma_start(note_pool[0][:], note_planes[0])
+        nc.sync.dma_start(note_pool[1][:], note_planes[1])
+        nc.sync.dma_start(list1[:], offs)
+        for q in range(4):
+            nc.sync.dma_start(
+                key_scale_pool[32 * q : 32 * q + 4, :].bitcast(I32),
+                keys_scales[0, 4 * q : 4 * q + 4, :].bitcast(I32),
+            )
+        nc.sync.dma_start(note_pool[2][:], note_planes[2])
+        nc.sync.dma_start(note_pool[3][:], note_planes[3])
+        nc.sync.dma_start(
+            key_pool[:].bitcast(I32), keys_words[0].rearrange("p n t -> p (n t)").bitcast(I32)
+        )
+        nc.sync.dma_start(list3[:], offs3)
+        nc.sync.dma_start(factor2[:], rowf2.rearrange("(p t) o -> p (t o)", t=PACK))
+        nc.sync.dma_start(factor1[:], rowf.rearrange("(p t) o -> p (t o)", t=PACK))
+        for b in range(BLOCKS):
+            nc.sync.dma_start(val2_pool[b][:], vals2[b * P : (b + 1) * P, :])
+        for b in range(BLOCKS):
+            nc.sync.dma_start(val_pool[b][:], vals[b * P : (b + 1) * P, :])
+        make_identity(nc, ident[:])
+
+        H = N // 2
+        halves = (slice(0, H), slice(H, N))
+        list_halves = (slice(0, H // 16), slice(H // 16, N // 16))
+        note_cols = staged("cols", [P, PACK, N], BF16, "note_cols")
+        gather(nc, False, note_cols[:, 0, :], note_pool[0][:], list2[:])
+        gather(nc, True, note_cols[:, 1, :], note_pool[1][:], list2[:])
+        key_scales = keep.tile([P, PACK, P], U8, name="key_scales", align_bytes=64)
+        nc.vector.tensor_copy(
+            key_scales[:].rearrange("p t s -> p s t"), key_scale_pool[:].indirect(list1[:])
+        )
+        gather(nc, False, note_cols[:, 2, :], note_pool[2][:], list2[:])
+        for h in range(2):
+            gather(nc, h == 0, note_cols[:, 3, halves[h]], note_pool[3][:], list2[:, list_halves[h]])
+        note_scales = keep.tile([P, N], U8, name="note_scales", align_bytes=64)
+        note_woven = []
+        for h in range(2):
+            woven = staged("woven%d" % h, [P, H, PACK], BF16, "note_woven%d" % h)
+            dst = woven[:].rearrange("p (c i) t -> p c t i", i=4)
+            src = note_cols[:, :, halves[h]].rearrange("p t (c i) -> p c t i", i=4)
+            if h == 0:
+                nc.vector.tensor_copy(dst, src)
+            else:
+                nc.scalar.copy(dst, src)
+            note_woven.append(woven[:].rearrange("p j t -> p (j t)"))
+        note_words = [staged("note_words0", [P, H], U32, "note_words0")]
+        quantise(nc, note_words[0][:], note_scales[:, halves[0]], note_woven[0])
+        key_words = staged("woven0", [P, PACK, P], U32, "key_words")
+        nc.vector.tensor_copy(
+            key_words[:].rearrange("p t s -> p s t"), key_pool[:].indirect(list1[:])
+        )
+        note_words.append(staged("key_pool", [P, H], U32, "note_words1"))
+        quantise(nc, note_words[1][:], note_scales[:, halves[1]], note_woven[1])
+
+        gr1 = keep.tile([P, N, PACK], BF16, name="gr1", align_bytes=64)
+        gr2 = keep.tile([P, N, PACK], BF16, name="gr2", align_bytes=64)
+        for c in range(BLOCKS):
+            cols = slice(c * P, (c + 1) * P)
+            table = bank(c, [P, PACK, P], "table%d" % c)
+            for t in range(PACK):
+                nc.tensor.matmul_mx(
+                    out=table[:, t, :],
+                    lhsT=key_words[:, t, :].bitcast(FP8X4),
+                    lhsT_scale=key_scales[:, t, :],
+                    rhs=note_words[c // 2][:, (c % 2) * P : (c % 2 + 1) * P].bitcast(FP8X4),
+                    rhs_scale=note_scales[:, cols],
+                    start=True,
+                    stop=True,
+                )
+            for gr, factor in ((gr2, factor2), (gr1, factor1)):
+                nc.vector.scalar_tensor_tensor(
+                    out=gr[:, cols, :],
+                    in0=table[:].rearrange("p t j -> p j t"),
+                    scalar=0.0,
+                    in1=factor[:].unsqueeze(1).to_broadcast([P, P, PACK]),
+                    op0=ALU.max,
+                    op1=ALU.mult,
+                )
+        gr_words = keep.tile([P, 2, N], U32, name="gr_words", align_bytes=64)
+        gr_scales = keep.tile([P, 2, N], U8, name="gr_scales", align_bytes=64)
+        quantise(nc, gr_words[:, 1, :], gr_scales[:, 1, :], gr2[:].rearrange("p j t -> p (j t)"))
+        quantise(nc, gr_words[:, 0, :], gr_scales[:, 0, :], gr1[:].rearrange("p j t -> p (j t)"))
+
+        def turn(turned, cols):
+            pairs = cols.bitcast(F32)
+            for u in range(2):
+                nc.tensor.transpose(turned[:, u, :], pairs[:, u::2], ident[:])
+
+        val2_cols = staged("cols", [P, BLOCKS, N], BF16, "val2_cols")
+        vt2_words = keep.tile([P, N], U32, name="vt2_words", align_bytes=64)
+        vt2_scales = keep.tile([P, N], U8, name="vt2_scales", align_bytes=64)
+        for b in range(BLOCKS):
+            gather(nc, False, val2_cols[:, b, :], val2_pool[b][:], list3[:])
+        vt2 = staged("vt2", [P, BLOCKS, P, PACK], BF16, "vt2")
+        for h in range(2):
+            turned = bank(h, [P, 2, 2, P], "turned2_%d" % h)
+            for k in range(2):
+                turn(turned[:, k], val2_cols[:, 2 * h + k, :])
+            nc.scalar.copy(
+                vt2[:, 2 * h : 2 * h + 2].bitcast(F32), turned[:].rearrange("p k u e -> p k e u")
+            )
+        quantise(nc, vt2_words[:], vt2_scales[:], vt2[:].rearrange("p b e t -> p (b e t)"))
+
+        pieces = [(b, slice(0, N), 4 + b) for b in range(BLOCKS - 1)]
+        pieces = pieces + [(BLOCKS - 1, halves[0], 7), (BLOCKS - 1, halves[1], 0)]
+        accs = [bank(number, [P, cols.stop - cols.start], "acc%d" % k) for k, (b, cols, number) in enumerate(pieces)]
+        vt1_words = {}
+        vt1_scales = keep.tile([P, N], U8, name="vt1_scales", align_bytes=64)
+
+        def product(k, store, start):
+            b, cols, number = pieces[k]
+            rows = slice(b * P, (b + 1) * P)
+            words = vt2_words[:, rows] if store == 1 else vt1_words[b][:]
+            scales = vt2_scales[:, rows] if store == 1 else vt1_scales[:, rows]
+            nc.tensor.matmul_mx(
+                out=accs[k][:],
+                lhsT=words.bitcast(FP8X4),
+                lhsT_scale=scales,
+                rhs=gr_words[:, store, cols].bitcast(FP8X4),
+                rhs_scale=gr_scales[:, store, cols],
+                start=start,
+                stop=not start,
+            )
+
+        turn_bank = (2, 3, 1, 2)
+
+        def fetch(b, tag):
+            val_cols = staged(tag, [P, N], BF16, "val_cols%d" % b)
+            if b == BLOCKS - 1:
+                for h in range(2):
+                    gather(nc, h == 0, val_cols[:, halves[h]], val_pool[b][:], list1[:, list_halves[h]])
+            else:
+                gather(nc, b > 0, val_cols[:], val_pool[b][:], list1[:])
+            turned = bank(turn_bank[b], [P, 2, P], "turned1_%d" % b)
+            turn(turned, val_cols[:])
+            vt1 = staged("vt1_%d" % b, [P, P, PACK], BF16, "vt1_%d" % b)
+            nc.scalar.copy(vt1[:].bitcast(F32), turned[:].rearrange("p u e -> p e u"))
+            return vt1
+
+        def quantise_vt1(b, vt1, tag):
+            vt1_words[b] = staged(tag, [P, P], U32, "vt1_words%d" % b)
+            quantise(
+                nc, vt1_words[b][:], vt1_scales[:, b * P : (b + 1) * P],
+                vt1[:].rearrange("p e t -> p (e t)"),
+            )
+
+        def store(k, on_vector, queue):
+            b, cols, number = pieces[k]
+            result = keep.tile([P, cols.stop - cols.start], F32, name="result%d" % k)
+            if on_vector:
+                nc.vector.tensor_copy(result[:], accs[k][:])
+            else:
+                nc.scalar.copy(result[:], accs[k][:])
+            queue.dma_start(out[b * P : (b + 1) * P, cols], result[:])
+
+        for k in (3, 4, 2):
+            product(k, 1, True)
+        vt1_0 = fetch(0, "cols")
+        vt1_1 = fetch(1, "vt2")
+        quantise_vt1(0, vt1_0, "val_pool1")
+        product(0, 0, True)
+        product(0, 1, False)
+        quantise_vt1(1, vt1_1, "vt1_words1")
+        product(1, 0, True)
+        product(1, 1, False)
+        store(0, False, nc.sync)
+        store(1, False, nc.sync)
+        vt1_2 = fetch(2, "vt1_1")
+        vt1_3 = fetch(3, "vt1_1")
+        quantise_vt1(2, vt1_2, "val_pool3")
+        product(2, 0, False)
+        quantise_vt1(3, vt1_3, "vt1_words3")
+        product(3, 0, False)
+        product(4, 0, False)
+        store(2, False, nc.sync)
+        store(3, True, nc.sync)
+        store(4, False, nc.scalar)

@@ -39,6 +39,7 @@ def tile_attend_tab_plain_twostores_kernel(
     nc = tc.nc
     with ExitStack() as ctx:
         keep = ctx.enter_context(tc.tile_pool(name="keep", bufs=1))
+        last = ctx.enter_context(tc.tile_pool(name="last", bufs=1))
         psum = ctx.enter_context(tc.psum_pool(name="psum", bufs=1))
 
         def bank(number, shape, name):
@@ -53,8 +54,9 @@ def tile_attend_tab_plain_twostores_kernel(
         note_pool = [keep.tile([P, U], F32, name="note_pool%d" % t) for t in range(PACK)]
         key_pool = staged("key_pool", [P, T], U32, "key_pool")
         key_scale_pool = keep.tile([P, T], U8, name="key_scale_pool")
-        val_pool = [staged("val_pool%d" % b, [P, T], F32, "val_pool%d" % b) for b in range(BLOCKS)]
-        val2_pool = [keep.tile([P, Y], F32, name="val2_pool%d" % b) for b in range(BLOCKS)]
+        val_pool = [staged("val_pool%d" % b, [P, T], F32, "val_pool%d" % b) for b in range(BLOCKS - 1)]
+        val_pool.append(last.tile([P, T], F32, name="val_pool3", offset=0, align_bytes=64))
+        val2_pool = [staged("val2_pool%d" % b, [P, Y], F32, "val2_pool%d" % b) for b in range(BLOCKS)]
         factor1 = keep.tile([P, PACK], F32, name="factor1")
         factor2 = keep.tile([P, PACK], F32, name="factor2")
         ident = keep.tile([P, P], F32, name="ident")
@@ -63,15 +65,14 @@ def tile_attend_tab_plain_twostores_kernel(
         note_planes = notes.rearrange("(p t) u -> t p u", t=PACK)
         nc.sync.dma_start(list2[:], offs2)
         nc.sync.dma_start(note_pool[0][:], note_planes[0])
-        nc.sync.dma_start(note_pool[1][:], note_planes[1])
         nc.sync.dma_start(list1[:], offs)
         for q in range(4):
             nc.sync.dma_start(
                 key_scale_pool[32 * q : 32 * q + 4, :].bitcast(I32),
                 keys_scales[0, 4 * q : 4 * q + 4, :].bitcast(I32),
             )
-        nc.sync.dma_start(note_pool[2][:], note_planes[2])
-        nc.sync.dma_start(note_pool[3][:], note_planes[3])
+        for t in range(1, PACK):
+            nc.sync.dma_start(note_pool[t][:], note_planes[t])
         nc.sync.dma_start(
             key_pool[:].bitcast(I32), keys_words[0].rearrange("p n t -> p (n t)").bitcast(I32)
         )
@@ -89,12 +90,12 @@ def tile_attend_tab_plain_twostores_kernel(
         list_halves = (slice(0, H // 16), slice(H // 16, N // 16))
         note_cols = staged("cols", [P, PACK, N], BF16, "note_cols")
         gather(nc, False, note_cols[:, 0, :], note_pool[0][:], list2[:])
-        gather(nc, True, note_cols[:, 1, :], note_pool[1][:], list2[:])
         key_scales = keep.tile([P, PACK, P], U8, name="key_scales", align_bytes=64)
         nc.vector.tensor_copy(
             key_scales[:].rearrange("p t s -> p s t"), key_scale_pool[:].indirect(list1[:])
         )
-        gather(nc, False, note_cols[:, 2, :], note_pool[2][:], list2[:])
+        for t in range(1, PACK - 1):
+            gather(nc, t % 2 == 1, note_cols[:, t, :], note_pool[t][:], list2[:])
         for h in range(2):
             gather(nc, h == 0, note_cols[:, 3, halves[h]], note_pool[3][:], list2[:, list_halves[h]])
         note_scales = keep.tile([P, N], U8, name="note_scales", align_bytes=64)
@@ -117,10 +118,8 @@ def tile_attend_tab_plain_twostores_kernel(
         note_words.append(staged("key_pool", [P, H], U32, "note_words1"))
         quantise(nc, note_words[1][:], note_scales[:, halves[1]], note_woven[1])
 
-        gr1 = keep.tile([P, N, PACK], BF16, name="gr1", align_bytes=64)
-        gr2 = keep.tile([P, N, PACK], BF16, name="gr2", align_bytes=64)
+        tables = []
         for c in range(BLOCKS):
-            cols = slice(c * P, (c + 1) * P)
             table = bank(c, [P, PACK, P], "table%d" % c)
             for t in range(PACK):
                 nc.tensor.matmul_mx(
@@ -128,66 +127,87 @@ def tile_attend_tab_plain_twostores_kernel(
                     lhsT=key_words[:, t, :].bitcast(FP8X4),
                     lhsT_scale=key_scales[:, t, :],
                     rhs=note_words[c // 2][:, (c % 2) * P : (c % 2 + 1) * P].bitcast(FP8X4),
-                    rhs_scale=note_scales[:, cols],
+                    rhs_scale=note_scales[:, c * P : (c + 1) * P],
                     start=True,
                     stop=True,
                 )
-            for gr, factor in ((gr2, factor2), (gr1, factor1)):
-                nc.vector.scalar_tensor_tensor(
-                    out=gr[:, cols, :],
-                    in0=table[:].rearrange("p t j -> p j t"),
-                    scalar=0.0,
-                    in1=factor[:].unsqueeze(1).to_broadcast([P, P, PACK]),
-                    op0=ALU.max,
-                    op1=ALU.mult,
-                )
-        gr_words = keep.tile([P, 2, N], U32, name="gr_words", align_bytes=64)
-        gr_scales = keep.tile([P, 2, N], U8, name="gr_scales", align_bytes=64)
-        quantise(nc, gr_words[:, 1, :], gr_scales[:, 1, :], gr2[:].rearrange("p j t -> p (j t)"))
-        quantise(nc, gr_words[:, 0, :], gr_scales[:, 0, :], gr1[:].rearrange("p j t -> p (j t)"))
+            tables.append(table)
+
+        def weigh(gr, table, factor):
+            nc.vector.scalar_tensor_tensor(
+                out=gr,
+                in0=table[:].rearrange("p t j -> p j t"),
+                scalar=0.0,
+                in1=factor[:].unsqueeze(1).to_broadcast([P, P, PACK]),
+                op0=ALU.max,
+                op1=ALU.mult,
+            )
 
         def turn(turned, cols):
             pairs = cols.bitcast(F32)
             for u in range(2):
                 nc.tensor.transpose(turned[:, u, :], pairs[:, u::2], ident[:])
 
-        val2_cols = staged("cols", [P, BLOCKS, N], BF16, "val2_cols")
-        vt2_words = keep.tile([P, N], U32, name="vt2_words", align_bytes=64)
-        vt2_scales = keep.tile([P, N], U8, name="vt2_scales", align_bytes=64)
-        for b in range(BLOCKS):
-            gather(nc, False, val2_cols[:, b, :], val2_pool[b][:], list3[:])
-        vt2 = staged("vt2", [P, BLOCKS, P, PACK], BF16, "vt2")
-        for h in range(2):
-            turned = bank(h, [P, 2, 2, P], "turned2_%d" % h)
-            for k in range(2):
-                turn(turned[:, k], val2_cols[:, 2 * h + k, :])
-            nc.scalar.copy(
-                vt2[:, 2 * h : 2 * h + 2].bitcast(F32), turned[:].rearrange("p k u e -> p k e u")
-            )
-        quantise(nc, vt2_words[:], vt2_scales[:], vt2[:].rearrange("p b e t -> p (b e t)"))
+        gr_words = keep.tile([P, 2, N], U32, name="gr_words", align_bytes=64)
+        gr_scales = keep.tile([P, 2, N], U8, name="gr_scales", align_bytes=64)
+        gr2 = keep.tile([P, N, PACK], BF16, name="gr2", align_bytes=64)
+        for c in range(BLOCKS):
+            weigh(gr2[:, c * P : (c + 1) * P, :], tables[c], factor2)
+        quantise(nc, gr_words[:, 1, :], gr_scales[:, 1, :], gr2[:].rearrange("p j t -> p (j t)"))
 
-        pieces = [(b, slice(0, N), 4 + b) for b in range(BLOCKS - 1)]
-        pieces = pieces + [(BLOCKS - 1, halves[0], 7), (BLOCKS - 1, halves[1], 0)]
-        accs = [bank(number, [P, cols.stop - cols.start], "acc%d" % k) for k, (b, cols, number) in enumerate(pieces)]
-        vt1_words = {}
-        vt1_scales = keep.tile([P, N], U8, name="vt1_scales", align_bytes=64)
+        pieces = [(0, slice(0, N), 6), (1, slice(0, N), 7), (2, slice(0, N), 0), (3, halves[0], 1), (3, halves[1], 4)]
+        accs = {}
+        vt_words = {}
+        vt_scales = keep.tile([P, 2, N], U8, name="vt_scales", align_bytes=64)
 
-        def product(k, store, start):
+        def product(k, store):
             b, cols, number = pieces[k]
-            rows = slice(b * P, (b + 1) * P)
-            words = vt2_words[:, rows] if store == 1 else vt1_words[b][:]
-            scales = vt2_scales[:, rows] if store == 1 else vt1_scales[:, rows]
+            if store == 1:
+                accs[k] = bank(number, [P, cols.stop - cols.start], "acc%d" % k)
             nc.tensor.matmul_mx(
                 out=accs[k][:],
-                lhsT=words.bitcast(FP8X4),
-                lhsT_scale=scales,
+                lhsT=vt_words[(store, b)].bitcast(FP8X4),
+                lhsT_scale=vt_scales[:, store, b * P : (b + 1) * P],
                 rhs=gr_words[:, store, cols].bitcast(FP8X4),
                 rhs_scale=gr_scales[:, store, cols],
-                start=start,
-                stop=not start,
+                start=(store == 1),
+                stop=(store == 0),
             )
 
-        turn_bank = (2, 3, 1, 2)
+        val2_cols = [
+            staged("cols" if b == 0 else "val2_cols%d" % b, [P, N], BF16, "val2_cols%d" % b)
+            for b in range(BLOCKS)
+        ]
+        for b in range(BLOCKS):
+            gather(nc, False, val2_cols[b][:], val2_pool[b][:], list3[:])
+
+        def turn2(h):
+            turned = bank(4 + h, [P, 2, 2, P], "turned2_%d" % h)
+            for k in range(2):
+                turn(turned[:, k], val2_cols[2 * h + k][:])
+            return turned
+
+        def weave2(h, turned, tag):
+            vt2 = staged(tag, [P, 2, P, PACK], BF16, "vt2_%d" % h)
+            nc.scalar.copy(vt2[:].bitcast(F32), turned[:].rearrange("p k u e -> p k e u"))
+            return vt2
+
+        def quantise2(h, vt2, tag):
+            words = staged(tag, [P, H], U32, "vt2_words%d" % h)
+            quantise(nc, words[:], vt_scales[:, 1, halves[h]], vt2[:].rearrange("p b e t -> p (b e t)"))
+            for k in range(2):
+                vt_words[(1, 2 * h + k)] = words[:, k * P : (k + 1) * P]
+
+        def weigh1(h, tag):
+            gr1 = staged(tag, [P, H, PACK], BF16, "gr1_%d" % h)
+            for k in range(2):
+                weigh(gr1[:, k * P : (k + 1) * P, :], tables[2 * h + k], factor1)
+            return gr1
+
+        def quantise_gr1(h, gr1):
+            quantise(nc, gr_words[:, 0, halves[h]], gr_scales[:, 0, halves[h]], gr1[:].rearrange("p j t -> p (j t)"))
+
+        turn_bank = (2, 3, 5, 2)
 
         def fetch(b, tag):
             val_cols = staged(tag, [P, N], BF16, "val_cols%d" % b)
@@ -198,45 +218,57 @@ def tile_attend_tab_plain_twostores_kernel(
                 gather(nc, b > 0, val_cols[:], val_pool[b][:], list1[:])
             turned = bank(turn_bank[b], [P, 2, P], "turned1_%d" % b)
             turn(turned, val_cols[:])
+            return turned
+
+        def weave1(b, turned):
             vt1 = staged("vt1_%d" % b, [P, P, PACK], BF16, "vt1_%d" % b)
             nc.scalar.copy(vt1[:].bitcast(F32), turned[:].rearrange("p u e -> p e u"))
             return vt1
 
-        def quantise_vt1(b, vt1, tag):
-            vt1_words[b] = staged(tag, [P, P], U32, "vt1_words%d" % b)
-            quantise(
-                nc, vt1_words[b][:], vt1_scales[:, b * P : (b + 1) * P],
-                vt1[:].rearrange("p e t -> p (e t)"),
-            )
+        def quantise1(b, vt1, words):
+            vt_words[(0, b)] = words[:]
+            quantise(nc, words[:], vt_scales[:, 0, b * P : (b + 1) * P], vt1[:].rearrange("p e t -> p (e t)"))
 
-        def store(k, on_vector, queue):
+        def store(k, on_vector, queue, result):
             b, cols, number = pieces[k]
-            result = keep.tile([P, cols.stop - cols.start], F32, name="result%d" % k)
             if on_vector:
                 nc.vector.tensor_copy(result[:], accs[k][:])
             else:
                 nc.scalar.copy(result[:], accs[k][:])
             queue.dma_start(out[b * P : (b + 1) * P, cols], result[:])
 
-        for k in (3, 4, 2):
-            product(k, 1, True)
-        vt1_0 = fetch(0, "cols")
-        vt1_1 = fetch(1, "vt2")
-        quantise_vt1(0, vt1_0, "val_pool1")
-        product(0, 0, True)
-        product(0, 1, False)
-        quantise_vt1(1, vt1_1, "vt1_words1")
-        product(1, 0, True)
-        product(1, 1, False)
-        store(0, False, nc.sync)
-        store(1, False, nc.sync)
-        vt1_2 = fetch(2, "vt1_1")
-        vt1_3 = fetch(3, "vt1_1")
-        quantise_vt1(2, vt1_2, "val_pool3")
-        product(2, 0, False)
-        quantise_vt1(3, vt1_3, "vt1_words3")
-        product(3, 0, False)
-        product(4, 0, False)
-        store(2, False, nc.sync)
-        store(3, True, nc.sync)
-        store(4, False, nc.scalar)
+        turned2 = [turn2(0), turn2(1)]
+        vt2_0 = weave2(0, turned2[0], "val2_pool2")
+        gr1_0 = weigh1(0, "gr1_0")
+        quantise2(0, vt2_0, "vt2_words0")
+        product(0, 1)
+        product(1, 1)
+        gr1_1 = weigh1(1, "val2_pool2")
+        quantise_gr1(0, gr1_0)
+        quantise_gr1(1, gr1_1)
+        turned1_0 = fetch(0, "val2_cols1")
+        vt2_1 = weave2(1, turned2[1], "val_pool0")
+        vt1_0 = weave1(0, turned1_0)
+        turned1_1 = fetch(1, "val2_pool2")
+        quantise2(1, vt2_1, "val_pool1")
+        for k in (2, 3, 4):
+            product(k, 1)
+        vt1_1 = weave1(1, turned1_1)
+        quantise1(0, vt1_0, staged("val2_pool2", [P, P], U32, "vt1_words0"))
+        product(0, 0)
+        store(0, False, nc.sync, keep.tile([P, N], F32, name="result0"))
+        turned1_2 = fetch(2, "vt1_0")
+        quantise1(1, vt1_1, staged("val_pool2", [P, P], U32, "vt1_words1"))
+        product(1, 0)
+        vt1_2 = weave1(2, turned1_2)
+        turned1_3 = fetch(3, "vt1_1")
+        quantise1(2, vt1_2, last.tile([P, P], U32, name="vt1_words2", offset=0, align_bytes=64))
+        store(1, True, nc.sync, last.tile([P, N], F32, name="result1", offset=2048, align_bytes=64))
+        vt1_3 = weave1(3, turned1_3)
+        product(2, 0)
+        quantise1(3, vt1_3, staged("vt1_words3", [P, P], U32, "vt1_words3"))
+        product(3, 0)
+        product(4, 0)
+        store(2, False, nc.sync, keep.tile([P, N], F32, name="result2"))
+        store(3, True, nc.sync, keep.tile([P, H], F32, name="result3"))
+        store(4, False, nc.scalar, keep.tile([P, H], F32, name="result4"))

@@ -39,7 +39,7 @@ def tile_attend_tab_plain_twostores_kernel(
     nc = tc.nc
     with ExitStack() as ctx:
         keep = ctx.enter_context(tc.tile_pool(name="keep", bufs=1))
-        last = ctx.enter_context(tc.tile_pool(name="last", bufs=1))
+        shared = ctx.enter_context(tc.tile_pool(name="shared", bufs=1))
         psum = ctx.enter_context(tc.psum_pool(name="psum", bufs=1))
 
         def bank(number, shape, name):
@@ -48,14 +48,16 @@ def tile_attend_tab_plain_twostores_kernel(
         def staged(tag, shape, dtype, name):
             return keep.tile(shape, dtype, name=name, tag=tag, align_bytes=64)
 
+        def tenant(b, byte, shape, dtype, name):
+            return shared.tile(shape, dtype, name=name, offset=b * T * 4 + byte, align_bytes=64)
+
         list1 = keep.tile([P, N // 16], U16, name="list1")
         list2 = keep.tile([P, N // 16], U16, name="list2")
         list3 = keep.tile([P, N // 16], U16, name="list3")
         note_pool = [keep.tile([P, U], F32, name="note_pool%d" % t) for t in range(PACK)]
         key_pool = staged("key_pool", [P, T], U32, "key_pool")
         key_scale_pool = keep.tile([P, T], U8, name="key_scale_pool")
-        val_pool = [staged("val_pool%d" % b, [P, T], F32, "val_pool%d" % b) for b in range(BLOCKS - 1)]
-        val_pool.append(last.tile([P, T], F32, name="val_pool3", offset=0, align_bytes=64))
+        val_pool = [tenant(b, 0, [P, T], F32, "val_pool%d" % b) for b in range(BLOCKS)]
         val2_pool = [staged("val2_pool%d" % b, [P, Y], F32, "val2_pool%d" % b) for b in range(BLOCKS)]
         factor1 = keep.tile([P, PACK], F32, name="factor1")
         factor2 = keep.tile([P, PACK], F32, name="factor2")
@@ -66,10 +68,9 @@ def tile_attend_tab_plain_twostores_kernel(
         nc.sync.dma_start(list2[:], offs2)
         nc.sync.dma_start(note_pool[0][:], note_planes[0])
         nc.sync.dma_start(list1[:], offs)
-        for q in range(4):
+        for r in range(4):
             nc.sync.dma_start(
-                key_scale_pool[32 * q : 32 * q + 4, :].bitcast(I32),
-                keys_scales[0, 4 * q : 4 * q + 4, :].bitcast(I32),
+                key_scale_pool[r:P:32, :].bitcast(I32), keys_scales[0, r:16:4, :].bitcast(I32)
             )
         for t in range(1, PACK):
             nc.sync.dma_start(note_pool[t][:], note_planes[t])
@@ -187,13 +188,11 @@ def tile_attend_tab_plain_twostores_kernel(
                 turn(turned[:, k], val2_cols[2 * h + k][:])
             return turned
 
-        def weave2(h, turned, tag):
-            vt2 = staged(tag, [P, 2, P, PACK], BF16, "vt2_%d" % h)
+        def weave2(turned, vt2):
             nc.scalar.copy(vt2[:].bitcast(F32), turned[:].rearrange("p k u e -> p k e u"))
             return vt2
 
-        def quantise2(h, vt2, tag):
-            words = staged(tag, [P, H], U32, "vt2_words%d" % h)
+        def quantise2(h, vt2, words):
             quantise(nc, words[:], vt_scales[:, 1, halves[h]], vt2[:].rearrange("p b e t -> p (b e t)"))
             for k in range(2):
                 vt_words[(1, 2 * h + k)] = words[:, k * P : (k + 1) * P]
@@ -209,19 +208,17 @@ def tile_attend_tab_plain_twostores_kernel(
 
         turn_bank = (2, 3, 5, 2)
 
-        def fetch(b, tag):
-            val_cols = staged(tag, [P, N], BF16, "val_cols%d" % b)
-            if b == BLOCKS - 1:
+        def fetch(b, val_cols):
+            if b > 0:
                 for h in range(2):
                     gather(nc, h == 0, val_cols[:, halves[h]], val_pool[b][:], list1[:, list_halves[h]])
             else:
-                gather(nc, b > 0, val_cols[:], val_pool[b][:], list1[:])
+                gather(nc, False, val_cols[:], val_pool[b][:], list1[:])
             turned = bank(turn_bank[b], [P, 2, P], "turned1_%d" % b)
             turn(turned, val_cols[:])
             return turned
 
-        def weave1(b, turned):
-            vt1 = staged("vt1_%d" % b, [P, P, PACK], BF16, "vt1_%d" % b)
+        def weave1(turned, vt1):
             nc.scalar.copy(vt1[:].bitcast(F32), turned[:].rearrange("p u e -> p e u"))
             return vt1
 
@@ -238,33 +235,33 @@ def tile_attend_tab_plain_twostores_kernel(
             queue.dma_start(out[b * P : (b + 1) * P, cols], result[:])
 
         turned2 = [turn2(0), turn2(1)]
-        vt2_0 = weave2(0, turned2[0], "val2_pool2")
+        vt2_0 = weave2(turned2[0], staged("val2_pool2", [P, 2, P, PACK], BF16, "vt2_0"))
         gr1_0 = weigh1(0, "gr1_0")
-        quantise2(0, vt2_0, "vt2_words0")
+        quantise2(0, vt2_0, staged("vt2_words0", [P, H], U32, "vt2_words0"))
         product(0, 1)
         product(1, 1)
         gr1_1 = weigh1(1, "val2_pool2")
         quantise_gr1(0, gr1_0)
         quantise_gr1(1, gr1_1)
-        turned1_0 = fetch(0, "val2_cols1")
-        vt2_1 = weave2(1, turned2[1], "val_pool0")
-        vt1_0 = weave1(0, turned1_0)
-        turned1_1 = fetch(1, "val2_pool2")
-        quantise2(1, vt2_1, "val_pool1")
+        turned1_0 = fetch(0, staged("val2_cols1", [P, N], BF16, "val_cols0"))
+        vt2_1 = weave2(turned2[1], tenant(0, 0, [P, 2, P, PACK], BF16, "vt2_1"))
+        turned1_1 = fetch(1, staged("val2_pool2", [P, N], BF16, "val_cols1"))
+        quantise2(1, vt2_1, tenant(1, 0, [P, H], U32, "vt2_words1"))
+        vt1_0 = weave1(turned1_0, tenant(1, 1024, [P, P, PACK], BF16, "vt1_0"))
         for k in (2, 3, 4):
             product(k, 1)
-        vt1_1 = weave1(1, turned1_1)
-        quantise1(0, vt1_0, staged("val2_pool2", [P, P], U32, "vt1_words0"))
+        quantise1(0, vt1_0, staged("vt1_words0", [P, P], U32, "vt1_words0"))
+        vt1_1 = weave1(turned1_1, staged("vt1_1", [P, P, PACK], BF16, "vt1_1"))
         product(0, 0)
-        store(0, False, nc.sync, keep.tile([P, N], F32, name="result0"))
-        turned1_2 = fetch(2, "vt1_0")
-        quantise1(1, vt1_1, staged("val_pool2", [P, P], U32, "vt1_words1"))
+        turned1_2 = fetch(2, tenant(1, 1024, [P, N], BF16, "val_cols2"))
+        quantise1(1, vt1_1, tenant(2, 0, [P, P], U32, "vt1_words1"))
+        store(0, False, nc.sync, tenant(2, 2048, [P, N], F32, "result0"))
         product(1, 0)
-        vt1_2 = weave1(2, turned1_2)
-        turned1_3 = fetch(3, "vt1_1")
-        quantise1(2, vt1_2, last.tile([P, P], U32, name="vt1_words2", offset=0, align_bytes=64))
-        store(1, True, nc.sync, last.tile([P, N], F32, name="result1", offset=2048, align_bytes=64))
-        vt1_3 = weave1(3, turned1_3)
+        vt1_2 = weave1(turned1_2, staged("vt1_2", [P, P, PACK], BF16, "vt1_2"))
+        turned1_3 = fetch(3, staged("vt1_1", [P, N], BF16, "val_cols3"))
+        quantise1(2, vt1_2, tenant(3, 0, [P, P], U32, "vt1_words2"))
+        store(1, True, nc.sync, tenant(3, 2048, [P, N], F32, "result1"))
+        vt1_3 = weave1(turned1_3, staged("vt1_3", [P, P, PACK], BF16, "vt1_3"))
         product(2, 0)
         quantise1(3, vt1_3, staged("vt1_words3", [P, P], U32, "vt1_words3"))
         product(3, 0)

@@ -156,7 +156,7 @@ def tile_attend_tab_plain_twostores_kernel(
             weigh(gr2[:, c * P : (c + 1) * P, :], tables[c], factor2)
         quantise(nc, gr_words[:, 1, :], gr_scales[:, 1, :], gr2[:].rearrange("p j t -> p (j t)"))
 
-        pieces = [(0, slice(0, N), 6), (1, slice(0, N), 7), (2, slice(0, N), 0), (3, halves[0], 1), (3, halves[1], 4)]
+        pieces = [(0, slice(0, N), 6), (1, slice(0, N), 2), (2, slice(0, N), 3), (3, halves[0], 1), (3, halves[1], 4)]
         accs = {}
         vt_words = {}
         vt_scales = keep.tile([P, 2, N], U8, name="vt_scales", align_bytes=64)
@@ -197,6 +197,10 @@ def tile_attend_tab_plain_twostores_kernel(
             for k in range(2):
                 vt_words[(1, 2 * h + k)] = words[:, k * P : (k + 1) * P]
 
+        def quantise2_block(b, vt2, words):
+            vt_words[(1, b)] = words[:]
+            quantise(nc, words[:], vt_scales[:, 1, b * P : (b + 1) * P], vt2[:, b % 2].rearrange("p e t -> p (e t)"))
+
         def weigh1(h, tag):
             gr1 = staged(tag, [P, H, PACK], BF16, "gr1_%d" % h)
             for k in range(2):
@@ -206,7 +210,7 @@ def tile_attend_tab_plain_twostores_kernel(
         def quantise_gr1(h, gr1):
             quantise(nc, gr_words[:, 0, halves[h]], gr_scales[:, 0, halves[h]], gr1[:].rearrange("p j t -> p (j t)"))
 
-        turn_bank = (2, 3, 5, 2)
+        turn_bank = (2, 3, 5, 7)
 
         def fetch(b, val_cols):
             if b > 0:
@@ -239,24 +243,26 @@ def tile_attend_tab_plain_twostores_kernel(
         gr1_0 = weigh1(0, "gr1_0")
         quantise2(0, vt2_0, staged("vt2_words0", [P, H], U32, "vt2_words0"))
         product(0, 1)
-        product(1, 1)
         gr1_1 = weigh1(1, "val2_pool2")
         quantise_gr1(0, gr1_0)
         quantise_gr1(1, gr1_1)
         turned1_0 = fetch(0, staged("val2_cols1", [P, N], BF16, "val_cols0"))
         vt2_1 = weave2(turned2[1], tenant(0, 0, [P, 2, P, PACK], BF16, "vt2_1"))
         turned1_1 = fetch(1, staged("val2_pool2", [P, N], BF16, "val_cols1"))
-        quantise2(1, vt2_1, tenant(1, 0, [P, H], U32, "vt2_words1"))
+        quantise2_block(2, vt2_1, tenant(1, 0, [P, P], U32, "vt2_words2"))
         vt1_0 = weave1(turned1_0, tenant(1, 1024, [P, P, PACK], BF16, "vt1_0"))
-        for k in (2, 3, 4):
-            product(k, 1)
+        product(1, 1)
         quantise1(0, vt1_0, staged("vt1_words0", [P, P], U32, "vt1_words0"))
         vt1_1 = weave1(turned1_1, staged("vt1_1", [P, P, PACK], BF16, "vt1_1"))
         product(0, 0)
+        product(2, 1)
         turned1_2 = fetch(2, tenant(1, 1024, [P, N], BF16, "val_cols2"))
         quantise1(1, vt1_1, tenant(2, 0, [P, P], U32, "vt1_words1"))
         store(0, False, nc.sync, tenant(2, 2048, [P, N], F32, "result0"))
         product(1, 0)
+        quantise2_block(3, vt2_1, tenant(1, 1024, [P, P], U32, "vt2_words3"))
+        product(3, 1)
+        product(4, 1)
         vt1_2 = weave1(turned1_2, staged("vt1_2", [P, P, PACK], BF16, "vt1_2"))
         turned1_3 = fetch(3, staged("vt1_1", [P, N], BF16, "val_cols3"))
         quantise1(2, vt1_2, tenant(3, 0, [P, P], U32, "vt1_words2"))

@@ -64,6 +64,8 @@ def tile_attend_tab_plain_twostores_kernel(
         ident = keep.tile([P, P], F32, name="ident")
 
         nc.gpsimd.memset(key_scale_pool[:].bitcast(I32), 0)
+        nc.gpsimd.dma_start(factor2[:], rowf2.rearrange("(p t) o -> p (t o)", t=PACK))
+        nc.gpsimd.dma_start(factor1[:], rowf.rearrange("(p t) o -> p (t o)", t=PACK))
         note_planes = notes.rearrange("(p t) u -> t p u", t=PACK)
         nc.sync.dma_start(list2[:], offs2)
         nc.sync.dma_start(note_pool[0][:], note_planes[0])
@@ -78,8 +80,6 @@ def tile_attend_tab_plain_twostores_kernel(
             key_pool[:].bitcast(I32), keys_words[0].rearrange("p n t -> p (n t)").bitcast(I32)
         )
         nc.sync.dma_start(list3[:], offs3)
-        nc.sync.dma_start(factor2[:], rowf2.rearrange("(p t) o -> p (t o)", t=PACK))
-        nc.sync.dma_start(factor1[:], rowf.rearrange("(p t) o -> p (t o)", t=PACK))
         for b in range(BLOCKS):
             nc.sync.dma_start(val2_pool[b][:], vals2[b * P : (b + 1) * P, :])
         for b in range(BLOCKS):

from contextlib import ExitStack

import concourse.mybir as mybir
from concourse.masks import make_identity

F32 = mybir.dt.float32
BF16 = mybir.dt.bfloat16
I32 = mybir.dt.int32
U32 = mybir.dt.uint32
U16 = mybir.dt.uint16
U8 = mybir.dt.uint8
FP8X4 = mybir.dt.float8_e4m3fn_x4
COPY = mybir.ActivationFunctionType.Copy
ALU = mybir.AluOpType

P = 128
PACK = 4
N = 512
T, U, Y = 2048, 1024, 1024
BLOCKS = N // P

FLOPS = 3 * 2 * N * N * N


def gather(nc, on_vector, out, window, offsets):
    if on_vector:
        nc.vector.tensor_copy(out, window.indirect(offsets))
    else:
        nc.scalar.activation(out, window.indirect(offsets), COPY)


def quantise(nc, words, scales, woven):
    nc.vector.quantize_mx(out=words.bitcast(FP8X4), scales=scales, in_=woven)


def tile_attend_tab_plain_twostores_kernel(
    tc, keys_words, keys_scales, notes, rowf, rowf2, vals, vals2, offs, offs2, offs3, out
):
    nc = tc.nc
    with ExitStack() as ctx:
        keep = ctx.enter_context(tc.tile_pool(name="keep", bufs=1))
        shared = ctx.enter_context(tc.tile_pool(name="shared", bufs=1))
        psum = ctx.enter_context(tc.psum_pool(name="psum", bufs=1))

        def bank(number, shape, name):
            return psum.tile(shape, F32, name=name, tag="bank%d" % number)

        def staged(tag, shape, dtype, name):
            return keep.tile(shape, dtype, name=name, tag=tag, align_bytes=64)

        def tenant(b, byte, shape, dtype, name):
            return shared.tile(shape, dtype, name=name, offset=b * T * 4 + byte, align_bytes=64)

        list1 = keep.tile([P, N // 16], U16, name="list1")
        list2 = keep.tile([P, N // 16], U16, name="list2")
        list3 = keep.tile([P, N // 16], U16, name="list3")
        note_pool = [keep.tile([P, U], F32, name="note_pool%d" % t) for t in range(PACK)]
        key_pool = staged("key_pool", [P, T], U32, "key_pool")
        key_scale_pool = keep.tile([P, T], U8, name="key_scale_pool")
        val_pool = [tenant(b, 0, [P, T], F32, "val_pool%d" % b) for b in range(BLOCKS)]
        val2_pool = [staged("val2_pool%d" % b, [P, Y], F32, "val2_pool%d" % b) for b in range(BLOCKS)]
        factor1 = keep.tile([P, PACK], F32, name="factor1")
        factor2 = keep.tile([P, PACK], F32, name="factor2")
        ident = keep.tile([P, P], F32, name="ident")

        nc.gpsimd.memset(key_scale_pool[:].bitcast(I32), 0)
        nc.gpsimd.dma_start(factor2[:], rowf2.rearrange("(p t) o -> p (t o)", t=PACK))
        nc.gpsimd.dma_start(factor1[:], rowf.rearrange("(p t) o -> p (t o)", t=PACK))
        note_planes = notes.rearrange("(p t) u -> t p u", t=PACK)
        nc.sync.dma_start(list2[:], offs2)
        nc.sync.dma_start(note_pool[0][:], note_planes[0])
        nc.sync.dma_start(list1[:], offs)
        for r in range(4):
            nc.sync.dma_start(
                key_scale_pool[r:P:32, :].bitcast(I32), keys_scales[0, r:16:4, :].bitcast(I32)
            )
        for t in range(1, PACK):
            nc.sync.dma_start(note_pool[t][:], note_planes[t])
        nc.sync.dma_start(
            key_pool[:].bitcast(I32), keys_words[0].rearrange("p n t -> p (n t)").bitcast(I32)
        )
        nc.sync.dma_start(list3[:], offs3)
        for b in range(BLOCKS):
            nc.sync.dma_start(val2_pool[b][:], vals2[b * P : (b + 1) * P, :])
        for b in range(BLOCKS):
            nc.sync.dma_start(val_pool[b][:], vals[b * P : (b + 1) * P, :])
        make_identity(nc, ident[:])

        H = N // 2
        halves = (slice(0, H), slice(H, N))
        list_halves = (slice(0, H // 16), slice(H // 16, N // 16))
        note_cols = staged("cols", [P, PACK, N], BF16, "note_cols")
        gather(nc, False, note_cols[:, 0, :], note_pool[0][:], list2[:])
        key_scales = keep.tile([P, PACK, P], U8, name="key_scales", align_bytes=64)
        nc.vector.tensor_copy(
            key_scales[:].rearrange("p t s -> p s t"), key_scale_pool[:].indirect(list1[:])
        )
        for t in range(1, PACK - 1):
            gather(nc, t % 2 == 1, note_cols[:, t, :], note_pool[t][:], list2[:])
        for h in range(2):
            gather(nc, h == 0, note_cols[:, 3, halves[h]], note_pool[3][:], list2[:, list_halves[h]])
        note_scales = keep.tile([P, N], U8, name="note_scales", align_bytes=64)
        note_woven = []
        for h in range(2):
            woven = staged("woven%d" % h, [P, H, PACK], BF16, "note_woven%d" % h)
            dst = woven[:].rearrange("p (c i) t -> p c t i", i=4)
            src = note_cols[:, :, halves[h]].rearrange("p t (c i) -> p c t i", i=4)
            if h == 0:
                nc.vector.tensor_copy(dst, src)
            else:
                nc.scalar.copy(dst, src)
            note_woven.append(woven[:].rearrange("p j t -> p (j t)"))
        note_words = [staged("note_words0", [P, H], U32, "note_words0")]
        quantise(nc, note_words[0][:], note_scales[:, halves[0]], note_woven[0])
        key_words = staged("woven0", [P, PACK, P], U32, "key_words")
        nc.vector.tensor_copy(
            key_words[:].rearrange("p t s -> p s t"), key_pool[:].indirect(list1[:])
        )
        note_words.append(staged("key_pool", [P, H], U32, "note_words1"))
        quantise(nc, note_words[1][:], note_scales[:, halves[1]], note_woven[1])

        tables = []
        for c in range(BLOCKS):
            table = bank(c, [P, PACK, P], "table%d" % c)
            for t in range(PACK):
                nc.tensor.matmul_mx(
                    out=table[:, t, :],
                    lhsT=key_words[:, t, :].bitcast(FP8X4),
                    lhsT_scale=key_scales[:, t, :],
                    rhs=note_words[c // 2][:, (c % 2) * P : (c % 2 + 1) * P].bitcast(FP8X4),
                    rhs_scale=note_scales[:, c * P : (c + 1) * P],
                    start=True,
                    stop=True,
                )
            tables.append(table)

        def weigh(gr, table, factor):
            nc.vector.scalar_tensor_tensor(
                out=gr,
                in0=table[:].rearrange("p t j -> p j t"),
                scalar=0.0,
                in1=factor[:].unsqueeze(1).to_broadcast([P, P, PACK]),
                op0=ALU.max,
                op1=ALU.mult,
            )

        def turn(turned, cols):
            pairs = cols.bitcast(F32)
            for u in range(2):
                nc.tensor.transpose(turned[:, u, :], pairs[:, u::2], ident[:])

        gr_words = keep.tile([P, 2, N], U32, name="gr_words", align_bytes=64)
        gr_scales = keep.tile([P, 2, N], U8, name="gr_scales", align_bytes=64)
        gr2 = keep.tile([P, N, PACK], BF16, name="gr2", align_bytes=64)
        for c in range(BLOCKS):
            weigh(gr2[:, c * P : (c + 1) * P, :], tables[c], factor2)
        quantise(nc, gr_words[:, 1, :], gr_scales[:, 1, :], gr2[:].rearrange("p j t -> p (j t)"))

        pieces = [(0, slice(0, N), 6), (1, slice(0, N), 2), (2, slice(0, N), 3), (3, halves[0], 1), (3, halves[1], 4)]
        accs = {}
        vt_words = {}
        vt_scales = keep.tile([P, 2, N], U8, name="vt_scales", align_bytes=64)

        def product(k, store):
            b, cols, number = pieces[k]
            if store == 1:
                accs[k] = bank(number, [P, cols.stop - cols.start], "acc%d" % k)
            nc.tensor.matmul_mx(
                out=accs[k][:],
                lhsT=vt_words[(store, b)].bitcast(FP8X4),
                lhsT_scale=vt_scales[:, store, b * P : (b + 1) * P],
                rhs=gr_words[:, store, cols].bitcast(FP8X4),
                rhs_scale=gr_scales[:, store, cols],
                start=(store == 1),
                stop=(store == 0),
            )

        val2_cols = [
            staged("cols" if b == 0 else "val2_cols%d" % b, [P, N], BF16, "val2_cols%d" % b)
            for b in range(BLOCKS)
        ]
        for b in range(BLOCKS):
            gather(nc, False, val2_cols[b][:], val2_pool[b][:], list3[:])

        def turn2(h):
            turned = bank(4 + h, [P, 2, 2, P], "turned2_%d" % h)
            for k in range(2):
                turn(turned[:, k], val2_cols[2 * h + k][:])
            return turned

        def weave2(turned, vt2):
            nc.scalar.copy(vt2[:].bitcast(F32), turned[:].rearrange("p k u e -> p k e u"))
            return vt2

        def quantise2(h, vt2, words):
            quantise(nc, words[:], vt_scales[:, 1, halves[h]], vt2[:].rearrange("p b e t -> p (b e t)"))
            for k in range(2):
                vt_words[(1, 2 * h + k)] = words[:, k * P : (k + 1) * P]

        def quantise2_block(b, vt2, words):
            vt_words[(1, b)] = words[:]
            quantise(nc, words[:], vt_scales[:, 1, b * P : (b + 1) * P], vt2[:, b % 2].rearrange("p e t -> p (e t)"))

        def weigh1(h, tag):
            gr1 = staged(tag, [P, H, PACK], BF16, "gr1_%d" % h)
            for k in range(2):
                weigh(gr1[:, k * P : (k + 1) * P, :], tables[2 * h + k], factor1)
            return gr1

        def quantise_gr1(h, gr1):
            quantise(nc, gr_words[:, 0, halves[h]], gr_scales[:, 0, halves[h]], gr1[:].rearrange("p j t -> p (j t)"))

        turn_bank = (2, 3, 5, 7)

        def fetch(b, val_cols):
            if b > 0:
                for h in range(2):
                    gather(nc, h == 0, val_cols[:, halves[h]], val_pool[b][:], list1[:, list_halves[h]])
            else:
                gather(nc, False, val_cols[:], val_pool[b][:], list1[:])
            turned = bank(turn_bank[b], [P, 2, P], "turned1_%d" % b)
            turn(turned, val_cols[:])
            return turned

        def weave1(turned, vt1):
            nc.scalar.copy(vt1[:].bitcast(F32), turned[:].rearrange("p u e -> p e u"))
            return vt1

        def quantise1(b, vt1, words):
            vt_words[(0, b)] = words[:]
            quantise(nc, words[:], vt_scales[:, 0, b * P : (b + 1) * P], vt1[:].rearrange("p e t -> p (e t)"))

        def store(k, on_vector, queue, result):
            b, cols, number = pieces[k]
            if on_vector:
                nc.vector.tensor_copy(result[:], accs[k][:])
            else:
                nc.scalar.copy(result[:], accs[k][:])
            queue.dma_start(out[b * P : (b + 1) * P, cols], result[:])

        turned2 = [turn2(0), turn2(1)]
        vt2_0 = weave2(turned2[0], staged("val2_pool2", [P, 2, P, PACK], BF16, "vt2_0"))
        gr1_0 = weigh1(0, "gr1_0")
        quantise2(0, vt2_0, staged("vt2_words0", [P, H], U32, "vt2_words0"))
        product(0, 1)
        gr1_1 = weigh1(1, "val2_pool2")
        quantise_gr1(0, gr1_0)
        quantise_gr1(1, gr1_1)
        turned1_0 = fetch(0, staged("val2_cols1", [P, N], BF16, "val_cols0"))
        vt2_1 = weave2(turned2[1], tenant(0, 0, [P, 2, P, PACK], BF16, "vt2_1"))
        turned1_1 = fetch(1, staged("val2_pool2", [P, N], BF16, "val_cols1"))
        quantise2_block(2, vt2_1, tenant(1, 0, [P, P], U32, "vt2_words2"))
        vt1_0 = weave1(turned1_0, tenant(1, 1024, [P, P, PACK], BF16, "vt1_0"))
        product(1, 1)
        quantise1(0, vt1_0, staged("vt1_words0", [P, P], U32, "vt1_words0"))
        vt1_1 = weave1(turned1_1, staged("vt1_1", [P, P, PACK], BF16, "vt1_1"))
        product(0, 0)
        product(2, 1)
        turned1_2 = fetch(2, tenant(1, 1024, [P, N], BF16, "val_cols2"))
        quantise1(1, vt1_1, tenant(2, 0, [P, P], U32, "vt1_words1"))
        store(0, False, nc.sync, tenant(2, 2048, [P, N], F32, "result0"))
        product(1, 0)
        quantise2_block(3, vt2_1, tenant(1, 1024, [P, P], U32, "vt2_words3"))
        product(3, 1)
        product(4, 1)
        vt1_2 = weave1(turned1_2, staged("vt1_2", [P, P, PACK], BF16, "vt1_2"))
        turned1_3 = fetch(3, staged("vt1_1", [P, N], BF16, "val_cols3"))
        quantise1(2, vt1_2, tenant(3, 0, [P, P], U32, "vt1_words2"))
        store(1, True, nc.sync, tenant(3, 2048, [P, N], F32, "result1"))
        vt1_3 = weave1(turned1_3, staged("vt1_3", [P, P, PACK], BF16, "vt1_3"))
        product(2, 0)
        quantise1(3, vt1_3, staged("vt1_words3", [P, P], U32, "vt1_words3"))
        product(3, 0)
        product(4, 0)
        store(2, False, nc.sync, keep.tile([P, N], F32, name="result2"))
        store(3, True, nc.sync, keep.tile([P, H], F32, name="result3"))
        store(4, False, nc.scalar, keep.tile([P, H], F32, name="result4"))
